import numpy as np
import ml_dtypes

BF16 = ml_dtypes.bfloat16


def bf(x):
    return np.asarray(x, np.float32).astype(BF16)


def f32(x):
    return np.asarray(x, np.float32)


def f64(x):
    return np.asarray(x).astype(np.float64)


def striped(idx):
    return np.tile(idx.reshape(-1, 16).T, (8, 1))


S, K, M, N = 512, 512, 512, 384


def setup_inputs():
    return {"base": bf(np.random.standard_normal((M, S))), "x": bf(np.random.standard_normal((K, N))), "w": bf(np.random.standard_normal((K, M)) / np.sqrt(K)), "offs": striped(np.random.permutation(S)[:N])}


def reference(base, x, w, offs):
    idx = offs[:16].T.reshape(-1)
    z = f64(base).copy()
    z[:, idx] += f64(w).T @ f64(x)
    return z

@@ -1,0 +1,51 @@
+import concourse.mybir as mybir
+from concourse.masks import make_identity
+
+BF16, F32, U16 = mybir.dt.bfloat16, mybir.dt.float32, mybir.dt.uint16
+
+P = 128
+M, K, S, N = 512, 512, 512, 384
+M_BLOCKS = M // P
+K_BLOCKS = K // P
+
+FLOPS = 2 * M * K * N
+
+
+def tile_scatter_matmul_kernel(tc, base, x, w, offs, out):
+    nc = tc.nc
+    with (
+        tc.tile_pool(name="held", bufs=1) as held,
+        tc.psum_pool(name="banks", bufs=1) as banks,
+    ):
+        offsets = held.tile([P, N // 16], U16, name="offsets")
+        nc.sync.dma_start(offsets[:], offs)
+
+        ident = held.tile([P, P], BF16, name="ident")
+        make_identity(nc, ident[:])
+
+        base_tiles = [held.tile([P, S], BF16, name=f"base{m}") for m in range(M_BLOCKS)]
+        w_tiles = [held.tile([P, M], BF16, name=f"w{k}") for k in range(K_BLOCKS)]
+        x_tiles = [held.tile([P, N], BF16, name=f"x{k}") for k in range(K_BLOCKS)]
+        for m in range(M_BLOCKS):
+            queue = nc.sync if m % 2 == 0 else nc.scalar
+            queue.dma_start(base_tiles[m][:], base[m * P : (m + 1) * P, :])
+        for k in range(K_BLOCKS):
+            nc.sync.dma_start(w_tiles[k][:], w[k * P : (k + 1) * P, :])
+            nc.scalar.dma_start(x_tiles[k][:], x[k * P : (k + 1) * P, :])
+
+        windows = [banks.tile([P, S], F32, name=f"window{m}") for m in range(M_BLOCKS)]
+        for m in range(M_BLOCKS):
+            nc.tensor.matmul(windows[m][:], ident[:], base_tiles[m][:], start=True, stop=False)
+
+        for m in range(M_BLOCKS):
+            for k in range(K_BLOCKS):
+                nc.tensor.matmul(
+                    windows[m][:].indirect(offsets[:]),
+                    w_tiles[k][:, m * P : (m + 1) * P],
+                    x_tiles[k][:],
+                    start=False,
+                    stop=(k == K_BLOCKS - 1),
+                )
+            staged = held.tile([P, S], F32, name=f"staged{m}")
+            nc.vector.tensor_copy(staged[:], windows[m][:])
+            nc.sync.dma_start(out[m * P : (m + 1) * P, :], staged[:])

@@ -7,6 +7,7 @@ P = 128
 M, K, S, N = 512, 512, 512, 384
 M_BLOCKS = M // P
 K_BLOCKS = K // P
+WARM_UPS = 4
 
 FLOPS = 2 * M * K * N
 
@@ -22,6 +23,12 @@ def tile_scatter_matmul_kernel(tc, base, x, w, offs, out):
 
         ident = held.tile([P, P], BF16, name="ident")
         make_identity(nc, ident[:])
+
+        zeros = held.tile([P, S], BF16, name="zeros")
+        nc.vector.memset(zeros[:], 0.0)
+        spare = banks.tile([P, S], F32, name="spare")
+        for i in range(WARM_UPS):
+            nc.tensor.matmul(spare[:], zeros[:, :P], zeros[:], start=True, stop=True)
 
         base_tiles = [held.tile([P, S], BF16, name=f"base{m}") for m in range(M_BLOCKS)]
         w_tiles = [held.tile([P, M], BF16, name=f"w{k}") for k in range(K_BLOCKS)]

@@ -44,8 +44,8 @@ def tile_scatter_matmul_kernel(tc, base, x, w, offs, out):
         for m in range(M_BLOCKS):
             nc.tensor.matmul(windows[m][:], ident[:], base_tiles[m][:], start=True, stop=False)
 
-        for m in range(M_BLOCKS):
-            for k in range(K_BLOCKS):
+        for k in range(K_BLOCKS):
+            for m in range(M_BLOCKS):
                 nc.tensor.matmul(
                     windows[m][:].indirect(offsets[:]),
                     w_tiles[k][:, m * P : (m + 1) * P],
@@ -53,6 +53,12 @@ def tile_scatter_matmul_kernel(tc, base, x, w, offs, out):
                     start=False,
                     stop=(k == K_BLOCKS - 1),
                 )
+
+        for m in range(M_BLOCKS):
             staged = held.tile([P, S], F32, name=f"staged{m}")
-            nc.vector.tensor_copy(staged[:], windows[m][:])
-            nc.sync.dma_start(out[m * P : (m + 1) * P, :], staged[:])
+            if m % 2 == 0:
+                nc.vector.tensor_copy(staged[:], windows[m][:])
+                nc.sync.dma_start(out[m * P : (m + 1) * P, :], staged[:])
+            else:
+                nc.scalar.copy(staged[:], windows[m][:])
+                nc.scalar.dma_start(out[m * P : (m + 1) * P, :], staged[:])

@@ -7,7 +7,8 @@ P = 128
 M, K, S, N = 512, 512, 512, 384
 M_BLOCKS = M // P
 K_BLOCKS = K // P
-WARM_UPS = 4
+HALF = S // 2
+WARM_UPS = 2
 
 FLOPS = 2 * M * K * N
 
@@ -18,9 +19,6 @@ def tile_scatter_matmul_kernel(tc, base, x, w, offs, out):
         tc.tile_pool(name="held", bufs=1) as held,
         tc.psum_pool(name="banks", bufs=1) as banks,
     ):
-        offsets = held.tile([P, N // 16], U16, name="offsets")
-        nc.sync.dma_start(offsets[:], offs)
-
         ident = held.tile([P, P], BF16, name="ident")
         make_identity(nc, ident[:])
 
@@ -36,6 +34,8 @@ def tile_scatter_matmul_kernel(tc, base, x, w, offs, out):
         for m in range(M_BLOCKS):
             queue = nc.sync if m % 2 == 0 else nc.scalar
             queue.dma_start(base_tiles[m][:], base[m * P : (m + 1) * P, :])
+        offsets = held.tile([P, N // 16], U16, name="offsets")
+        nc.sync.dma_start(offsets[:], offs)
         for k in range(K_BLOCKS):
             nc.sync.dma_start(w_tiles[k][:], w[k * P : (k + 1) * P, :])
             nc.scalar.dma_start(x_tiles[k][:], x[k * P : (k + 1) * P, :])
@@ -44,8 +44,8 @@ def tile_scatter_matmul_kernel(tc, base, x, w, offs, out):
         for m in range(M_BLOCKS):
             nc.tensor.matmul(windows[m][:], ident[:], base_tiles[m][:], start=True, stop=False)
 
-        for k in range(K_BLOCKS):
-            for m in range(M_BLOCKS):
+        for m in range(M_BLOCKS):
+            for k in range(K_BLOCKS):
                 nc.tensor.matmul(
                     windows[m][:].indirect(offsets[:]),
                     w_tiles[k][:, m * P : (m + 1) * P],
@@ -53,12 +53,9 @@ def tile_scatter_matmul_kernel(tc, base, x, w, offs, out):
                     start=False,
                     stop=(k == K_BLOCKS - 1),
                 )
-
-        for m in range(M_BLOCKS):
-            staged = held.tile([P, S], F32, name=f"staged{m}")
-            if m % 2 == 0:
-                nc.vector.tensor_copy(staged[:], windows[m][:])
-                nc.sync.dma_start(out[m * P : (m + 1) * P, :], staged[:])
-            else:
-                nc.scalar.copy(staged[:], windows[m][:])
-                nc.scalar.dma_start(out[m * P : (m + 1) * P, :], staged[:])
+            left = held.tile([P, HALF], F32, name=f"left{m}")
+            right = held.tile([P, HALF], F32, name=f"right{m}")
+            nc.vector.tensor_copy(left[:], windows[m][:, :HALF])
+            nc.sync.dma_start(out[m * P : (m + 1) * P, :HALF], left[:])
+            nc.vector.tensor_copy(right[:], windows[m][:, HALF:])
+            nc.scalar.dma_start(out[m * P : (m + 1) * P, HALF:], right[:])

@@ -44,15 +44,21 @@ def tile_scatter_matmul_kernel(tc, base, x, w, offs, out):
         for m in range(M_BLOCKS):
             nc.tensor.matmul(windows[m][:], ident[:], base_tiles[m][:], start=True, stop=False)
 
+        def add_at_listed_places(m, k):
+            nc.tensor.matmul(
+                windows[m][:].indirect(offsets[:]),
+                w_tiles[k][:, m * P : (m + 1) * P],
+                x_tiles[k][:],
+                start=False,
+                stop=(k == K_BLOCKS - 1),
+            )
+
         for m in range(M_BLOCKS):
-            for k in range(K_BLOCKS):
-                nc.tensor.matmul(
-                    windows[m][:].indirect(offsets[:]),
-                    w_tiles[k][:, m * P : (m + 1) * P],
-                    x_tiles[k][:],
-                    start=False,
-                    stop=(k == K_BLOCKS - 1),
-                )
+            add_at_listed_places(m, 0)
+
+        for m in range(M_BLOCKS):
+            for k in range(1, K_BLOCKS):
+                add_at_listed_places(m, k)
             left = held.tile([P, HALF], F32, name=f"left{m}")
             right = held.tile([P, HALF], F32, name=f"right{m}")
             nc.vector.tensor_copy(left[:], windows[m][:, :HALF])

@@ -32,13 +32,12 @@ def tile_scatter_matmul_kernel(tc, base, x, w, offs, out):
         w_tiles = [held.tile([P, M], BF16, name=f"w{k}") for k in range(K_BLOCKS)]
         x_tiles = [held.tile([P, N], BF16, name=f"x{k}") for k in range(K_BLOCKS)]
         for m in range(M_BLOCKS):
-            queue = nc.sync if m % 2 == 0 else nc.scalar
-            queue.dma_start(base_tiles[m][:], base[m * P : (m + 1) * P, :])
+            nc.sync.dma_start(base_tiles[m][:], base[m * P : (m + 1) * P, :])
         offsets = held.tile([P, N // 16], U16, name="offsets")
         nc.sync.dma_start(offsets[:], offs)
         for k in range(K_BLOCKS):
+            nc.sync.dma_start(x_tiles[k][:], x[k * P : (k + 1) * P, :])
             nc.sync.dma_start(w_tiles[k][:], w[k * P : (k + 1) * P, :])
-            nc.scalar.dma_start(x_tiles[k][:], x[k * P : (k + 1) * P, :])
 
         windows = [banks.tile([P, S], F32, name=f"window{m}") for m in range(M_BLOCKS)]
         for m in range(M_BLOCKS):

@@ -63,4 +63,4 @@ def tile_scatter_matmul_kernel(tc, base, x, w, offs, out):
             nc.vector.tensor_copy(left[:], windows[m][:, :HALF])
             nc.sync.dma_start(out[m * P : (m + 1) * P, :HALF], left[:])
             nc.vector.tensor_copy(right[:], windows[m][:, HALF:])
-            nc.scalar.dma_start(out[m * P : (m + 1) * P, HALF:], right[:])
+            nc.sync.dma_start(out[m * P : (m + 1) * P, HALF:], right[:])

@@ -30,14 +30,23 @@ def tile_scatter_matmul_kernel(tc, base, x, w, offs, out):
 
         base_tiles = [held.tile([P, S], BF16, name=f"base{m}") for m in range(M_BLOCKS)]
         w_tiles = [held.tile([P, M], BF16, name=f"w{k}") for k in range(K_BLOCKS)]
+        w_head = held.tile([P, P], BF16, name="w_head")
         x_tiles = [held.tile([P, N], BF16, name=f"x{k}") for k in range(K_BLOCKS)]
         for m in range(M_BLOCKS):
             nc.sync.dma_start(base_tiles[m][:], base[m * P : (m + 1) * P, :])
         offsets = held.tile([P, N // 16], U16, name="offsets")
         nc.sync.dma_start(offsets[:], offs)
-        for k in range(K_BLOCKS):
+        nc.sync.dma_start(x_tiles[0][:], x[:P, :])
+        nc.sync.dma_start(w_head[:], w[:P, :P])
+        nc.sync.dma_start(w_tiles[0][:, P:], w[:P, P:])
+        for k in range(1, K_BLOCKS):
             nc.sync.dma_start(x_tiles[k][:], x[k * P : (k + 1) * P, :])
             nc.sync.dma_start(w_tiles[k][:], w[k * P : (k + 1) * P, :])
+
+        def weights(m, k):
+            if m == 0 and k == 0:
+                return w_head[:]
+            return w_tiles[k][:, m * P : (m + 1) * P]
 
         windows = [banks.tile([P, S], F32, name=f"window{m}") for m in range(M_BLOCKS)]
         for m in range(M_BLOCKS):
@@ -46,7 +55,7 @@ def tile_scatter_matmul_kernel(tc, base, x, w, offs, out):
         def add_at_listed_places(m, k):
             nc.tensor.matmul(
                 windows[m][:].indirect(offsets[:]),
-                w_tiles[k][:, m * P : (m + 1) * P],
+                weights(m, k),
                 x_tiles[k][:],
                 start=False,
                 stop=(k == K_BLOCKS - 1),

@@ -9,6 +9,7 @@ M_BLOCKS = M // P
 K_BLOCKS = K // P
 HALF = S // 2
 WARM_UPS = 2
+DMA_ALIGN = 256
 
 FLOPS = 2 * M * K * N
 
@@ -28,10 +29,10 @@ def tile_scatter_matmul_kernel(tc, base, x, w, offs, out):
         for i in range(WARM_UPS):
             nc.tensor.matmul(spare[:], zeros[:, :P], zeros[:], start=True, stop=True)
 
-        base_tiles = [held.tile([P, S], BF16, name=f"base{m}") for m in range(M_BLOCKS)]
-        w_tiles = [held.tile([P, M], BF16, name=f"w{k}") for k in range(K_BLOCKS)]
-        w_head = held.tile([P, P], BF16, name="w_head")
-        x_tiles = [held.tile([P, N], BF16, name=f"x{k}") for k in range(K_BLOCKS)]
+        base_tiles = [held.tile([P, S], BF16, name=f"base{m}", align_bytes=DMA_ALIGN) for m in range(M_BLOCKS)]
+        w_tiles = [held.tile([P, M], BF16, name=f"w{k}", align_bytes=DMA_ALIGN) for k in range(K_BLOCKS)]
+        w_head = held.tile([P, P], BF16, name="w_head", align_bytes=DMA_ALIGN)
+        x_tiles = [held.tile([P, N], BF16, name=f"x{k}", align_bytes=DMA_ALIGN) for k in range(K_BLOCKS)]
         for m in range(M_BLOCKS):
             nc.sync.dma_start(base_tiles[m][:], base[m * P : (m + 1) * P, :])
         offsets = held.tile([P, N // 16], U16, name="offsets")
@@ -67,8 +68,8 @@ def tile_scatter_matmul_kernel(tc, base, x, w, offs, out):
         for m in range(M_BLOCKS):
             for k in range(1, K_BLOCKS):
                 add_at_listed_places(m, k)
-            left = held.tile([P, HALF], F32, name=f"left{m}")
-            right = held.tile([P, HALF], F32, name=f"right{m}")
+            left = held.tile([P, HALF], F32, name=f"left{m}", align_bytes=DMA_ALIGN)
+            right = held.tile([P, HALF], F32, name=f"right{m}", align_bytes=DMA_ALIGN)
             nc.vector.tensor_copy(left[:], windows[m][:, :HALF])
             nc.sync.dma_start(out[m * P : (m + 1) * P, :HALF], left[:])
             nc.vector.tensor_copy(right[:], windows[m][:, HALF:])

@@ -35,7 +35,7 @@ def tile_scatter_matmul_kernel(tc, base, x, w, offs, out):
         x_tiles = [held.tile([P, N], BF16, name=f"x{k}", align_bytes=DMA_ALIGN) for k in range(K_BLOCKS)]
         for m in range(M_BLOCKS):
             nc.sync.dma_start(base_tiles[m][:], base[m * P : (m + 1) * P, :])
-        offsets = held.tile([P, N // 16], U16, name="offsets")
+        offsets = held.tile([P, N // 16], U16, name="offsets", align_bytes=DMA_ALIGN)
         nc.sync.dma_start(offsets[:], offs)
         nc.sync.dma_start(x_tiles[0][:], x[:P, :])
         nc.sync.dma_start(w_head[:], w[:P, :P])

@@ -7,7 +7,8 @@ P = 128
 M, K, S, N = 512, 512, 512, 384
 M_BLOCKS = M // P
 K_BLOCKS = K // P
-HALF = S // 2
+PIECES = 2
+LAST_PIECES = 4
 WARM_UPS = 2
 DMA_ALIGN = 256
 
@@ -68,9 +69,10 @@ def tile_scatter_matmul_kernel(tc, base, x, w, offs, out):
         for m in range(M_BLOCKS):
             for k in range(1, K_BLOCKS):
                 add_at_listed_places(m, k)
-            left = held.tile([P, HALF], F32, name=f"left{m}", align_bytes=DMA_ALIGN)
-            right = held.tile([P, HALF], F32, name=f"right{m}", align_bytes=DMA_ALIGN)
-            nc.vector.tensor_copy(left[:], windows[m][:, :HALF])
-            nc.sync.dma_start(out[m * P : (m + 1) * P, :HALF], left[:])
-            nc.vector.tensor_copy(right[:], windows[m][:, HALF:])
-            nc.sync.dma_start(out[m * P : (m + 1) * P, HALF:], right[:])
+            pieces = LAST_PIECES if m == M_BLOCKS - 1 else PIECES
+            width = S // pieces
+            for i in range(pieces):
+                columns = slice(i * width, (i + 1) * width)
+                staged = held.tile([P, width], F32, name=f"staged{m}_{i}", align_bytes=DMA_ALIGN)
+                nc.vector.tensor_copy(staged[:], windows[m][:, columns])
+                nc.sync.dma_start(out[m * P : (m + 1) * P, columns], staged[:])

import concourse.mybir as mybir
from concourse.masks import make_identity

BF16, F32, U16 = mybir.dt.bfloat16, mybir.dt.float32, mybir.dt.uint16

P = 128
M, K, S, N = 512, 512, 512, 384
M_BLOCKS = M // P
K_BLOCKS = K // P
PIECES = 2
LAST_PIECES = 4
WARM_UPS = 2
DMA_ALIGN = 256

FLOPS = 2 * M * K * N


def tile_scatter_matmul_kernel(tc, base, x, w, offs, out):
    nc = tc.nc
    with (
        tc.tile_pool(name="held", bufs=1) as held,
        tc.psum_pool(name="banks", bufs=1) as banks,
    ):
        ident = held.tile([P, P], BF16, name="ident")
        make_identity(nc, ident[:])

        zeros = held.tile([P, S], BF16, name="zeros")
        nc.vector.memset(zeros[:], 0.0)
        spare = banks.tile([P, S], F32, name="spare")
        for i in range(WARM_UPS):
            nc.tensor.matmul(spare[:], zeros[:, :P], zeros[:], start=True, stop=True)

        base_tiles = [held.tile([P, S], BF16, name=f"base{m}", align_bytes=DMA_ALIGN) for m in range(M_BLOCKS)]
        w_tiles = [held.tile([P, M], BF16, name=f"w{k}", align_bytes=DMA_ALIGN) for k in range(K_BLOCKS)]
        w_head = held.tile([P, P], BF16, name="w_head", align_bytes=DMA_ALIGN)
        x_tiles = [held.tile([P, N], BF16, name=f"x{k}", align_bytes=DMA_ALIGN) for k in range(K_BLOCKS)]
        for m in range(M_BLOCKS):
            nc.sync.dma_start(base_tiles[m][:], base[m * P : (m + 1) * P, :])
        offsets = held.tile([P, N // 16], U16, name="offsets", align_bytes=DMA_ALIGN)
        nc.sync.dma_start(offsets[:], offs)
        nc.sync.dma_start(x_tiles[0][:], x[:P, :])
        nc.sync.dma_start(w_head[:], w[:P, :P])
        nc.sync.dma_start(w_tiles[0][:, P:], w[:P, P:])
        for k in range(1, K_BLOCKS):
            nc.sync.dma_start(x_tiles[k][:], x[k * P : (k + 1) * P, :])
            nc.sync.dma_start(w_tiles[k][:], w[k * P : (k + 1) * P, :])

        def weights(m, k):
            if m == 0 and k == 0:
                return w_head[:]
            return w_tiles[k][:, m * P : (m + 1) * P]

        windows = [banks.tile([P, S], F32, name=f"window{m}") for m in range(M_BLOCKS)]
        for m in range(M_BLOCKS):
            nc.tensor.matmul(windows[m][:], ident[:], base_tiles[m][:], start=True, stop=False)

        def add_at_listed_places(m, k):
            nc.tensor.matmul(
                windows[m][:].indirect(offsets[:]),
                weights(m, k),
                x_tiles[k][:],
                start=False,
                stop=(k == K_BLOCKS - 1),
            )

        for m in range(M_BLOCKS):
            add_at_listed_places(m, 0)

        for m in range(M_BLOCKS):
            for k in range(1, K_BLOCKS):
                add_at_listed_places(m, k)
            pieces = LAST_PIECES if m == M_BLOCKS - 1 else PIECES
            width = S // pieces
            for i in range(pieces):
                columns = slice(i * width, (i + 1) * width)
                staged = held.tile([P, width], F32, name=f"staged{m}_{i}", align_bytes=DMA_ALIGN)
                nc.vector.tensor_copy(staged[:], windows[m][:, columns])
                nc.sync.dma_start(out[m * P : (m + 1) * P, columns], staged[:])
